import numpy as np
import ml_dtypes


def mxq(x, axis, fmt="e4m3"):
    dtype, down = {"e4m3": (ml_dtypes.float8_e4m3fn, 7), "e5m2": (ml_dtypes.float8_e5m2, 14)}[fmt]
    v = np.moveaxis(np.asarray(x, np.float32).astype(ml_dtypes.bfloat16).astype(np.float64), axis, -1)
    blocks = v.reshape(v.shape[:-1] + (-1, 32))
    amax = np.abs(blocks).max(-1, keepdims=True)
    byte = np.maximum(np.where(amax > 0, np.frexp(amax)[1] - 1 + 127, 0) - down, 1)
    scale = np.exp2(byte - 127.0)
    codes = (blocks / scale).astype(np.float32).astype(dtype).astype(np.float64)
    return np.moveaxis((codes * scale).reshape(v.shape), -1, axis)


WIDE = False


def mx_kscale(k):
    if not WIDE:
        return np.ones(k)
    levels = np.array([10, -10, 5, -5, 0])
    if k % 512:
        return np.exp2(np.random.permutation(np.resize(levels, k // 32))).repeat(32)
    a = np.empty((k // 512, 16))
    for p in range(k // 512):
        a[p, :8] = np.random.permutation(np.resize(levels, 8))
        for g in range(8):
            far = levels[np.abs(levels - a[p, g]) >= 10]
            a[p, g + 8] = far[np.random.randint(len(far))]
    return np.exp2(a.ravel()).repeat(32)


BF16 = ml_dtypes.bfloat16


def bf(x):
    return np.asarray(x, np.float32).astype(BF16)


def f64(x):
    return np.asarray(x).astype(np.float64)


E2M1 = np.array([0.0, 0.5, 1.0, 1.5, 2.0, 3.0, 4.0, 6.0, -0.0, -0.5, -1.0, -1.5, -2.0, -3.0, -4.0, -6.0])


def pack_weight(w, fmt):
    k, n = w.shape
    w = f64(bf(w)).reshape(k // 32, 32, n)
    amax = np.abs(w).max(1)
    if fmt == "e4m3":
        byte = np.frexp(amax)[1] - 1 + 127 - 7
    else:
        mant, ex = np.frexp(amax / 6.0)
        byte = np.where(mant > 0.5, ex, ex - 1) + 127
    byte = np.clip(np.where(amax > 0, byte, 1), 1, 254)
    scaled = (w * np.exp2(127.0 - byte)[:, None, :]).reshape(k, n).astype(np.float32)
    by_word = np.ascontiguousarray(scaled.reshape(k // 512, 128, 4, n).transpose(0, 1, 3, 2))
    if fmt == "e4m3":
        words = by_word.astype(ml_dtypes.float8_e4m3fn).view(np.uint8)
    else:
        c = by_word.astype(ml_dtypes.float4_e2m1fn).view(np.uint8) & 0xF
        words = c[..., 0::2] | (c[..., 1::2] << 4)
    return np.ascontiguousarray(words), np.ascontiguousarray(byte.astype(np.uint8).reshape(k // 512, 16, n))


def unpack_weight(words, scales, fmt):
    g, p, n, _ = words.shape
    if fmt == "e4m3":
        vals = np.ascontiguousarray(words).view(ml_dtypes.float8_e4m3fn).astype(np.float64)
    else:
        nib = np.empty((g, p, n, 4), np.uint8)
        nib[..., 0::2] = words & 0xF
        nib[..., 1::2] = words >> 4
        vals = E2M1[nib]
    vals = vals * np.repeat(np.exp2(scales.astype(np.float64) - 127.0), 8, axis=1)[..., None]
    return vals.transpose(0, 1, 3, 2).reshape(g * 512, n)
def pack4(w):
    words, scales = pack_weight(w, "e2m1")
    return words.reshape(words.shape[0], 128, -1), scales


def unpack4(words, scales):
    return unpack_weight(words.reshape(words.shape[0], 128, -1, 2), scales, "e2m1")


M, KA, KB, N = 512, 512, 1536, 2048

FLOOR = 0.25
RHO = 1.5


def setup_inputs():
    s1, s2, t = mx_kscale(KA), mx_kscale(KB), mx_kscale(N)
    v = np.random.standard_normal((N, N)) / np.sqrt(N)
    v_rest_words, v_rest_scales = pack4(v[KA:] / s2[:, None] * t)
    vt_words, vt_scales = pack4(v.T / t[:, None])
    return {"x_top": bf(np.random.standard_normal((M, KA)) * s1),
            "x_rest": bf(np.random.standard_normal((M, KB)) * s2),
            "v_top": bf(v[:KA] / s1[:, None] * t),
            "v_rest_words": v_rest_words,
            "v_rest_scales": v_rest_scales,
            "lam": bf(0.5 + np.random.standard_normal(N)),
            "vt_words": vt_words,
            "vt_scales": vt_scales,
            "y": bf(np.random.standard_normal((M, N)))}


def reference(x_top, x_rest, v_top, v_rest_words, v_rest_scales, lam, vt_words, vt_scales, y):
    c = ((mxq(f64(x_top), 1, "e4m3") @ mxq(f64(v_top), 0, "e4m3"))
         + (mxq(f64(x_rest), 1, "e4m3") @ unpack4(v_rest_words, v_rest_scales)))
    h = c * np.maximum(f64(lam), FLOOR)
    z = mxq(h, 1, "e4m3") @ unpack4(vt_words, vt_scales)
    return RHO * (z - y)

@@ -1,0 +1,294 @@
+from contextlib import ExitStack
+
+import concourse.mybir as mybir
+from concourse.masks import make_identity
+
+M, KA, KB, N = 512, 512, 1536, 2048
+FLOOR = 0.25
+RHO = 1.5
+FLOPS = 2 * M * (KA + KB) * N + 2 * M * N * N
+
+F32 = mybir.dt.float32
+BF16 = mybir.dt.bfloat16
+I32 = mybir.dt.int32
+U32 = mybir.dt.uint32
+U8 = mybir.dt.uint8
+FP8X4 = mybir.dt.float8_e4m3fn_x4
+FP4X4 = mybir.dt.float4_e2m1fn_x4
+ALU = mybir.AluOpType
+ACT = mybir.ActivationFunctionType
+
+P = 128
+W = 512
+MT = M // P
+NC = N // W
+GR = KB // W
+
+
+def tile_psd_projection_dual_residual_s3_kernel(
+    tc, x_top, x_rest, v_top, v_rest_words, v_rest_scales, lam, vt_words, vt_scales, y, out
+):
+    nc = tc.nc
+    with ExitStack() as ctx:
+        keep = ctx.enter_context(tc.tile_pool(name="keep", bufs=1))
+        stage = ctx.enter_context(tc.tile_pool(name="stage", bufs=2))
+        outs = ctx.enter_context(tc.tile_pool(name="outs", bufs=4))
+        psum = ctx.enter_context(tc.psum_pool(name="psum", bufs=8))
+        ctx.enter_context(tc.manual_schedule())
+
+        def kept(name, shape, dtype):
+            return keep.tile(shape, dtype, name=name, align_bytes=64)
+
+        def bank():
+            return psum.tile([P, W], F32, name="bank")
+
+        lam_raw = kept("lam_raw", [P, 16], BF16)
+        lam_clip = kept("lam_clip", [P, 16], BF16)
+        lam_all = kept("lam_all", [P, N], BF16)
+        ident = kept("ident", [P, P], F32)
+        xr = [kept("xr%d" % m, [P, KB], BF16) for m in range(MT)]
+        xt = [kept("xt%d" % m, [P, KA], BF16) for m in range(MT)]
+        x_codes = [kept("xc%d" % m, [P, W], U32) for m in range(MT)]
+        x_scales = [kept("xs%d" % m, [P, W], U8) for m in range(MT)]
+        v_raw = [kept("vraw%d" % c, [P, 4, W], BF16) for c in range(NC)]
+        v_codes = [kept("vc%d" % c, [P, W], U32) for c in range(NC)]
+        v_scales = [kept("vs%d" % c, [P, W], U8) for c in range(NC)]
+        vr = [kept("vr%d" % c, [P, GR, 2 * W], U8) for c in range(NC)]
+        vr_plane_first = kept("vrs_first", [P, GR, W], U8)
+        vr_plane_later = kept("vrs_later", [P, GR, N - W], U8)
+        vt = [kept("vt%d" % g, [P, 2 * N], U8) for g in range(NC)]
+        vt_plane = kept("vts", [P, NC, N], U8)
+        h = [[kept("h%d_%d" % (c, m), [P, W], BF16) for m in range(MT)] for c in range(NC)]
+        h_codes = [kept("hc%d" % c, [P, W], U32) for c in range(NC)]
+        h_scales = [kept("hs%d" % c, [P, W], U8) for c in range(NC)]
+        y_raw = [kept("y%d" % m, [P, N], BF16) for m in range(MT)]
+        y_rho = [[kept("yr%d_%d" % (m, half), [P, N // 2], F32) for half in range(2)] for m in range(MT)]
+
+        nc.vector.memset(vr_plane_first[:].rearrange("p g n -> p (g n)").bitcast(I32), 0)
+        make_identity(nc, ident[:])
+        nc.gpsimd.memset(vr_plane_later[:].rearrange("p g n -> p (g n)").bitcast(I32), 0)
+        nc.gpsimd.memset(vt_plane[:].rearrange("p g n -> p (g n)").bitcast(I32), 0)
+
+        def load_x(m):
+            rows = slice(m * P, (m + 1) * P)
+            nc.sync.dma_start(out=xr[m][:], in_=x_rest[rows, :])
+            nc.sync.dma_start(out=xt[m][:], in_=x_top[rows, :])
+
+        def load_v_top(c):
+            nc.sync.dma_start(
+                out=v_raw[c][:], in_=v_top.rearrange("(p j) n -> p j n", j=4)[:, :, c * W : (c + 1) * W]
+            )
+
+        def load_v_rest(c):
+            nc.sync.dma_start(
+                out=vr[c][:].bitcast(I32),
+                in_=v_rest_words.bitcast(I32).rearrange("g p n -> p g n")[:, :, c * W // 2 : (c + 1) * W // 2],
+            )
+
+        def load_plane(plane, scales, first, last):
+            for r in range(4):
+                nc.sync.dma_start(
+                    out=plane[:].bitcast(I32)[r:P:32, :, :],
+                    in_=scales.bitcast(I32)[:, r:16:4, first // 4 : last // 4].rearrange("g q n -> q g n"),
+                )
+
+        nc.sync.dma_start(out=lam_raw[:], in_=lam.rearrange("(p c) -> p c", c=16))
+        load_x(0)
+        load_v_top(0)
+        load_x(1)
+        load_plane(vr_plane_first, v_rest_scales, 0, W)
+        load_v_rest(0)
+        load_x(2)
+        load_x(3)
+        load_v_top(1)
+        load_plane(vr_plane_later, v_rest_scales, W, N)
+        load_v_rest(1)
+        for c in range(2, NC):
+            load_v_top(c)
+            load_v_rest(c)
+        load_plane(vt_plane, vt_scales, 0, N)
+        nc.sync.dma_start(out=y_raw[0][:], in_=y[0:P, :])
+        for g in range(NC):
+            nc.sync.dma_start(out=vt[g][:].bitcast(I32), in_=vt_words.bitcast(I32)[g])
+        for m in range(1, MT):
+            nc.sync.dma_start(out=y_raw[m][:], in_=y[m * P : (m + 1) * P, :])
+
+        def turn_x(m):
+            grouped = stage.tile([P, 4 * W], BF16, name="xg", align_bytes=64)
+            sources = [xr[m][:].bitcast(F32)[:, 256 * g : 256 * (g + 1)] for g in range(GR)] + [xt[m][:].bitcast(F32)]
+            banks = [bank(), bank()]
+            for g in range(4):
+                for u in range(2):
+                    col = ((g % 2) * 2 + u) * P
+                    nc.tensor.transpose(banks[g // 2][:, col : col + P], sources[g][:, u:256:2], ident[:])
+            for b in range(2):
+                nc.scalar.copy(
+                    out=grouped[:].bitcast(F32)[:, b * W : (b + 1) * W].rearrange("p (g r u) -> p g r u", g=2, u=2),
+                    in_=banks[b][:].rearrange("p (g u r) -> p g r u", g=2, u=2),
+                )
+            return grouped
+
+        def quantize(codes, scales, grouped):
+            nc.vector.quantize_mx(out=codes[:].bitcast(FP8X4), scales=scales[:], in_=grouped[:])
+
+        def interleave_v(c, on_vector):
+            grouped = stage.tile([P, 4 * W], BF16, name="vg", align_bytes=64)
+            dst = grouped[:].rearrange("p (c i t) -> p c t i", i=4, t=4)
+            src = v_raw[c][:].rearrange("p t (c i) -> p c t i", i=4)
+            if on_vector:
+                nc.vector.tensor_copy(out=dst, in_=src)
+            else:
+                nc.scalar.copy(out=dst, in_=src)
+            return grouped
+
+        def spread_lam():
+            words = lam_clip[:].bitcast(F32)
+            banks = [bank(), bank()]
+            for u in range(2):
+                for b in range(4):
+                    w = 2 * b + u
+                    nc.tensor.transpose(
+                        banks[u][:, b * P : (b + 1) * P], words[:, w : w + 1].to_broadcast([P, P]), ident[:]
+                    )
+            for u in range(2):
+                nc.scalar.copy(
+                    out=lam_all[:].bitcast(F32).rearrange("p (c u a b) -> p u c a b", c=NC, u=2, b=4)[:, u],
+                    in_=banks[u][:].rearrange("p (b c a) -> p c a b", b=4, c=NC),
+                )
+
+        def first_stage(c, m):
+            acc = bank()
+            for g in range(4):
+                cols = slice(g * P, (g + 1) * P)
+                if g < GR:
+                    rhs = vr[c][:, g, :].bitcast(FP4X4)
+                    if c == 0:
+                        rhs_scale = vr_plane_first[:, g, :]
+                    else:
+                        rhs_scale = vr_plane_later[:, g, (c - 1) * W : c * W]
+                else:
+                    rhs = v_codes[c][:].bitcast(FP8X4)
+                    rhs_scale = v_scales[c][:]
+                nc.tensor.matmul_mx(
+                    out=acc[:],
+                    lhsT=x_codes[m][:, cols].bitcast(FP8X4),
+                    lhsT_scale=x_scales[m][:, cols],
+                    rhs=rhs,
+                    rhs_scale=rhs_scale,
+                    start=(g == 0),
+                    stop=(g == 3),
+                )
+            return acc
+
+        def weigh(c, m, acc):
+            nc.vector.tensor_tensor(
+                out=h[c][m][:].rearrange("p (u q e) -> p u q e", u=2, e=2),
+                in0=acc[:].rearrange("p (q u e) -> p u q e", u=2, e=2),
+                in1=lam_all[:, c * W : (c + 1) * W].rearrange("p (u q e) -> p u q e", u=2, e=2),
+                op=ALU.mult,
+            )
+
+        def turn_h(c):
+            grouped = stage.tile([P, 4 * W], BF16, name="hg", align_bytes=64)
+            banks = [bank(), bank()]
+            for m in range(MT):
+                for u in range(2):
+                    col = ((m % 2) * 2 + u) * P
+                    nc.tensor.transpose(
+                        banks[m // 2][:, col : col + P], h[c][m][:].bitcast(F32)[:, u * P : (u + 1) * P], ident[:]
+                    )
+            for b in range(2):
+                nc.scalar.copy(
+                    out=grouped[:].bitcast(F32)[:, b * W : (b + 1) * W].rearrange("p (g r u) -> p g r u", g=2, u=2),
+                    in_=banks[b][:].rearrange("p (g u r) -> p g r u", g=2, u=2),
+                )
+            return grouped
+
+        def scale_y(m):
+            for half in range(2):
+                nc.scalar.activation(
+                    out=y_rho[m][half][:],
+                    in_=y_raw[m][:, half * (N // 2) : (half + 1) * (N // 2)],
+                    func=ACT.Copy,
+                    scale=RHO,
+                )
+
+        def second_pass(acc, m, j, g):
+            cols = slice(m * P, (m + 1) * P)
+            nc.tensor.matmul_mx(
+                out=acc[:],
+                lhsT=h_codes[g][:, cols].bitcast(FP8X4),
+                lhsT_scale=h_scales[g][:, cols],
+                rhs=vt[g][:, 2 * j * W : 2 * (j + 1) * W].bitcast(FP4X4),
+                rhs_scale=vt_plane[:, g, j * W : (j + 1) * W],
+                start=(g == 0),
+                stop=(g == NC - 1),
+            )
+
+        def finish(acc, m, j):
+            result = outs.tile([P, W], F32, name="result")
+            nc.vector.scalar_tensor_tensor(
+                out=result[:],
+                in0=acc[:],
+                scalar=RHO,
+                in1=y_rho[m][j // 2][:, (j % 2) * W : (j % 2 + 1) * W],
+                op0=ALU.mult,
+                op1=ALU.subtract,
+            )
+            nc.sync.dma_start(out=out[m * P : (m + 1) * P, j * W : (j + 1) * W], in_=result[:])
+
+        nc.vector.tensor_scalar(out=lam_clip[:], in0=lam_raw[:], scalar1=FLOOR, scalar2=None, op0=ALU.max)
+        xg0 = turn_x(0)
+        spread_lam()
+        vg0 = interleave_v(0, True)
+        quantize(x_codes[0], x_scales[0], xg0)
+        quantize(v_codes[0], v_scales[0], vg0)
+        xg1 = turn_x(1)
+        quantize(x_codes[1], x_scales[1], xg1)
+        acc0 = first_stage(0, 0)
+        acc1 = first_stage(0, 1)
+        weigh(0, 0, acc0)
+        xg2 = turn_x(2)
+        xg3 = turn_x(3)
+        weigh(0, 1, acc1)
+        vg1 = interleave_v(1, True)
+        quantize(x_codes[2], x_scales[2], xg2)
+        quantize(v_codes[1], v_scales[1], vg1)
+        quantize(x_codes[3], x_scales[3], xg3)
+        for m in range(2, MT):
+            weigh(0, m, first_stage(0, m))
+
+        for c in range(1, NC):
+            if c + 1 < NC:
+                vg = interleave_v(c + 1, False)
+            weigh(c, 0, first_stage(c, 0))
+            weigh(c, 1, first_stage(c, 1))
+            hg = turn_h(c - 1)
+            if c + 1 < NC:
+                quantize(v_codes[c + 1], v_scales[c + 1], vg)
+            else:
+                scale_y(0)
+            weigh(c, 2, first_stage(c, 2))
+            quantize(h_codes[c - 1], h_scales[c - 1], hg)
+            weigh(c, 3, first_stage(c, 3))
+
+        accs = []
+        for j in range(NC):
+            if j == 2:
+                hg = turn_h(NC - 1)
+                quantize(h_codes[NC - 1], h_scales[NC - 1], hg)
+                scale_y(1)
+            accs.append(bank())
+            for g in range(NC - 1):
+                second_pass(accs[j], 0, j, g)
+        for j in range(NC):
+            second_pass(accs[j], 0, j, NC - 1)
+            finish(accs[j], 0, j)
+        for m in range(1, MT):
+            if m + 1 < MT:
+                scale_y(m + 1)
+            for j in range(NC):
+                acc = bank()
+                for g in range(NC):
+                    second_pass(acc, m, j, g)
+                finish(acc, m, j)

@@ -32,47 +32,57 @@ def tile_psd_projection_dual_residual_s3_kernel(
     with ExitStack() as ctx:
         keep = ctx.enter_context(tc.tile_pool(name="keep", bufs=1))
         stage = ctx.enter_context(tc.tile_pool(name="stage", bufs=2))
-        outs = ctx.enter_context(tc.tile_pool(name="outs", bufs=4))
-        psum = ctx.enter_context(tc.psum_pool(name="psum", bufs=8))
+        outs = ctx.enter_context(tc.tile_pool(name="outs", bufs=10))
+        psum = ctx.enter_context(tc.psum_pool(name="psum", bufs=1))
         ctx.enter_context(tc.manual_schedule())
 
         def kept(name, shape, dtype):
             return keep.tile(shape, dtype, name=name, align_bytes=64)
 
+        free_banks = list(range(8))
+
         def bank():
-            return psum.tile([P, W], F32, name="bank")
+            number = free_banks[0]
+            free_banks.remove(number)
+            return number, psum.tile([P, W], F32, name="bank%d" % number)
+
+        def release(held):
+            free_banks.append(held[0])
 
         lam_raw = kept("lam_raw", [P, 16], BF16)
         lam_clip = kept("lam_clip", [P, 16], BF16)
         lam_all = kept("lam_all", [P, N], BF16)
         ident = kept("ident", [P, P], F32)
         xr = [kept("xr%d" % m, [P, KB], BF16) for m in range(MT)]
-        xt = [kept("xt%d" % m, [P, KA], BF16) for m in range(MT)]
-        x_codes = [kept("xc%d" % m, [P, W], U32) for m in range(MT)]
-        x_scales = [kept("xs%d" % m, [P, W], U8) for m in range(MT)]
+        xt = kept("xt", [P, MT * KA], BF16)
+        xr_codes = [[kept("xc%d_%d" % (m, b), [P, (2 - b) * P], U32) for b in range(2)] for m in range(MT)]
+        xr_scales = [[kept("xs%d_%d" % (m, b), [P, (2 - b) * P], U8) for b in range(2)] for m in range(MT)]
+        xt_codes = [kept("xtc%d" % b, [P, 2 * P], U32) for b in range(2)]
+        xt_scales = [kept("xts%d" % b, [P, 2 * P], U8) for b in range(2)]
         v_raw = [kept("vraw%d" % c, [P, 4, W], BF16) for c in range(NC)]
         v_codes = [kept("vc%d" % c, [P, W], U32) for c in range(NC)]
         v_scales = [kept("vs%d" % c, [P, W], U8) for c in range(NC)]
         vr = [kept("vr%d" % c, [P, GR, 2 * W], U8) for c in range(NC)]
-        vr_plane_first = kept("vrs_first", [P, GR, W], U8)
-        vr_plane_later = kept("vrs_later", [P, GR, N - W], U8)
+        vr_planes = [kept("vrs%d" % i, [P, GR, width], U8) for i, width in enumerate((W, W, 2 * W))]
         vt = [kept("vt%d" % g, [P, 2 * N], U8) for g in range(NC)]
         vt_plane = kept("vts", [P, NC, N], U8)
         h = [[kept("h%d_%d" % (c, m), [P, W], BF16) for m in range(MT)] for c in range(NC)]
-        h_codes = [kept("hc%d" % c, [P, W], U32) for c in range(NC)]
-        h_scales = [kept("hs%d" % c, [P, W], U8) for c in range(NC)]
+        h_codes = [[kept("hc%d_%d" % (c, b), [P, 2 * P], U32) for b in range(2)] for c in range(NC)]
+        h_scales = [[kept("hs%d_%d" % (c, b), [P, 2 * P], U8) for b in range(2)] for c in range(NC)]
         y_raw = [kept("y%d" % m, [P, N], BF16) for m in range(MT)]
         y_rho = [[kept("yr%d_%d" % (m, half), [P, N // 2], F32) for half in range(2)] for m in range(MT)]
 
-        nc.vector.memset(vr_plane_first[:].rearrange("p g n -> p (g n)").bitcast(I32), 0)
-        make_identity(nc, ident[:])
-        nc.gpsimd.memset(vr_plane_later[:].rearrange("p g n -> p (g n)").bitcast(I32), 0)
-        nc.gpsimd.memset(vt_plane[:].rearrange("p g n -> p (g n)").bitcast(I32), 0)
+        def quantize(codes, scales, grouped):
+            nc.vector.quantize_mx(out=codes[:].bitcast(FP8X4), scales=scales[:], in_=grouped[:])
 
-        def load_x(m):
-            rows = slice(m * P, (m + 1) * P)
-            nc.sync.dma_start(out=xr[m][:], in_=x_rest[rows, :])
-            nc.sync.dma_start(out=xt[m][:], in_=x_top[rows, :])
+        def clear(plane):
+            nc.vector.memset(plane[:, :, :].rearrange("p g n -> p (g n)").bitcast(I32), 0)
+
+        make_identity(nc, ident[:])
+        clear(vr_planes[0])
+        clear(vr_planes[1])
+        clear(vr_planes[2])
+        clear(vt_plane[:, 0:2, :])
 
         def load_v_top(c):
             nc.sync.dma_start(
@@ -93,19 +103,25 @@ def tile_psd_projection_dual_residual_s3_kernel(
                 )
 
         nc.sync.dma_start(out=lam_raw[:], in_=lam.rearrange("(p c) -> p c", c=16))
-        load_x(0)
-        load_v_top(0)
-        load_x(1)
-        load_plane(vr_plane_first, v_rest_scales, 0, W)
+        nc.vector.tensor_scalar(out=lam_clip[:], in0=lam_raw[:], scalar1=FLOOR, scalar2=None, op0=ALU.max)
+        clear(vt_plane[:, 2:4, :])
+
+        def load_x_rest(m):
+            nc.sync.dma_start(out=xr[m][:], in_=x_rest[m * P : (m + 1) * P, :])
+
+        load_x_rest(0)
+        load_x_rest(1)
+        load_plane(vr_planes[0], v_rest_scales, 0, W)
         load_v_rest(0)
-        load_x(2)
-        load_x(3)
-        load_v_top(1)
-        load_plane(vr_plane_later, v_rest_scales, W, N)
-        load_v_rest(1)
-        for c in range(2, NC):
-            load_v_top(c)
+        load_x_rest(2)
+        load_x_rest(3)
+        nc.sync.dma_start(out=xt[:].rearrange("p (m k) -> p m k", m=MT), in_=x_top.rearrange("(m p) k -> p m k", p=P))
+        load_v_top(0)
+        for c in range(1, NC):
+            if c < 3:
+                load_plane(vr_planes[c], v_rest_scales, c * W, N if c == 2 else (c + 1) * W)
             load_v_rest(c)
+            load_v_top(c)
         load_plane(vt_plane, vt_scales, 0, N)
         nc.sync.dma_start(out=y_raw[0][:], in_=y[0:P, :])
         for g in range(NC):
@@ -113,23 +129,35 @@ def tile_psd_projection_dual_residual_s3_kernel(
         for m in range(1, MT):
             nc.sync.dma_start(out=y_raw[m][:], in_=y[m * P : (m + 1) * P, :])
 
-        def turn_x(m):
-            grouped = stage.tile([P, 4 * W], BF16, name="xg", align_bytes=64)
-            sources = [xr[m][:].bitcast(F32)[:, 256 * g : 256 * (g + 1)] for g in range(GR)] + [xt[m][:].bitcast(F32)]
-            banks = [bank(), bank()]
-            for g in range(4):
-                for u in range(2):
-                    col = ((g % 2) * 2 + u) * P
-                    nc.tensor.transpose(banks[g // 2][:, col : col + P], sources[g][:, u:256:2], ident[:])
-            for b in range(2):
-                nc.scalar.copy(
-                    out=grouped[:].bitcast(F32)[:, b * W : (b + 1) * W].rearrange("p (g r u) -> p g r u", g=2, u=2),
-                    in_=banks[b][:].rearrange("p (g u r) -> p g r u", g=2, u=2),
-                )
-            return grouped
+        def sort_words(raw, blocks):
+            ordered = stage.tile([P, 2, blocks * P], F32, name="ordered", align_bytes=64, bufs=3)
+            nc.vector.tensor_copy(
+                out=ordered[:].rearrange("p u (a i) -> p a u i", i=4),
+                in_=raw[:].bitcast(F32).rearrange("p (a i u) -> p a u i", i=4, u=2),
+            )
+            return [[ordered[:, u, s * P : (s + 1) * P] for u in range(2)] for s in range(blocks)]
 
-        def quantize(codes, scales, grouped):
-            nc.vector.quantize_mx(out=codes[:].bitcast(FP8X4), scales=scales[:], in_=grouped[:])
+        def turn(sources):
+            banks = [bank(), bank()]
+            for s in range(len(sources)):
+                for u in range(2):
+                    col = ((s % 2) * 2 + u) * P
+                    nc.tensor.transpose(banks[s // 2][1][:, col : col + P], sources[s][u], ident[:])
+            groups = []
+            for b in range(2):
+                blocks = min(2, len(sources) - 2 * b)
+                grouped = stage.tile([P, blocks * W], BF16, name="grouped", align_bytes=64, bufs=6)
+                nc.scalar.copy(
+                    out=grouped[:].bitcast(F32).rearrange("p (s r u) -> p s r u", s=blocks, u=2),
+                    in_=banks[b][1][:, 0 : blocks * 2 * P].rearrange("p (s u r) -> p s r u", s=blocks, u=2),
+                )
+                release(banks[b])
+                groups.append(grouped)
+            return groups
+
+        def quantize_pair(codes, scales, groups):
+            for b in range(2):
+                quantize(codes[b], scales[b], groups[b])
 
         def interleave_v(c, on_vector):
             grouped = stage.tile([P, 4 * W], BF16, name="vg", align_bytes=64)
@@ -148,61 +176,56 @@ def tile_psd_projection_dual_residual_s3_kernel(
                 for b in range(4):
                     w = 2 * b + u
                     nc.tensor.transpose(
-                        banks[u][:, b * P : (b + 1) * P], words[:, w : w + 1].to_broadcast([P, P]), ident[:]
+                        banks[u][1][:, b * P : (b + 1) * P], words[:, w : w + 1].to_broadcast([P, P]), ident[:]
                     )
             for u in range(2):
                 nc.scalar.copy(
                     out=lam_all[:].bitcast(F32).rearrange("p (c u a b) -> p u c a b", c=NC, u=2, b=4)[:, u],
-                    in_=banks[u][:].rearrange("p (b c a) -> p c a b", b=4, c=NC),
+                    in_=banks[u][1][:].rearrange("p (b c a) -> p c a b", b=4, c=NC),
                 )
+                release(banks[u])
 
-        def first_stage(c, m):
+        def rest_passes(c, m):
             acc = bank()
-            for g in range(4):
-                cols = slice(g * P, (g + 1) * P)
-                if g < GR:
-                    rhs = vr[c][:, g, :].bitcast(FP4X4)
-                    if c == 0:
-                        rhs_scale = vr_plane_first[:, g, :]
-                    else:
-                        rhs_scale = vr_plane_later[:, g, (c - 1) * W : c * W]
-                else:
-                    rhs = v_codes[c][:].bitcast(FP8X4)
-                    rhs_scale = v_scales[c][:]
+            plane = vr_planes[min(c, 2)]
+            first = W if c == 3 else 0
+            for g in range(GR):
+                cols = slice((g % 2) * P, (g % 2 + 1) * P)
                 nc.tensor.matmul_mx(
-                    out=acc[:],
-                    lhsT=x_codes[m][:, cols].bitcast(FP8X4),
-                    lhsT_scale=x_scales[m][:, cols],
-                    rhs=rhs,
-                    rhs_scale=rhs_scale,
+                    out=acc[1][:],
+                    lhsT=xr_codes[m][g // 2][:, cols].bitcast(FP8X4),
+                    lhsT_scale=xr_scales[m][g // 2][:, cols],
+                    rhs=vr[c][:, g, :].bitcast(FP4X4),
+                    rhs_scale=plane[:, g, first : first + W],
                     start=(g == 0),
-                    stop=(g == 3),
+                    stop=False,
                 )
             return acc
+
+        def top_pass(c, m, acc):
+            cols = slice((m % 2) * P, (m % 2 + 1) * P)
+            nc.tensor.matmul_mx(
+                out=acc[1][:],
+                lhsT=xt_codes[m // 2][:, cols].bitcast(FP8X4),
+                lhsT_scale=xt_scales[m // 2][:, cols],
+                rhs=v_codes[c][:].bitcast(FP8X4),
+                rhs_scale=v_scales[c][:],
+                start=False,
+                stop=True,
+            )
+            weigh(c, m, acc)
 
         def weigh(c, m, acc):
             nc.vector.tensor_tensor(
                 out=h[c][m][:].rearrange("p (u q e) -> p u q e", u=2, e=2),
-                in0=acc[:].rearrange("p (q u e) -> p u q e", u=2, e=2),
+                in0=acc[1][:].rearrange("p (q u e) -> p u q e", u=2, e=2),
                 in1=lam_all[:, c * W : (c + 1) * W].rearrange("p (u q e) -> p u q e", u=2, e=2),
                 op=ALU.mult,
             )
+            release(acc)
 
         def turn_h(c):
-            grouped = stage.tile([P, 4 * W], BF16, name="hg", align_bytes=64)
-            banks = [bank(), bank()]
-            for m in range(MT):
-                for u in range(2):
-                    col = ((m % 2) * 2 + u) * P
-                    nc.tensor.transpose(
-                        banks[m // 2][:, col : col + P], h[c][m][:].bitcast(F32)[:, u * P : (u + 1) * P], ident[:]
-                    )
-            for b in range(2):
-                nc.scalar.copy(
-                    out=grouped[:].bitcast(F32)[:, b * W : (b + 1) * W].rearrange("p (g r u) -> p g r u", g=2, u=2),
-                    in_=banks[b][:].rearrange("p (g u r) -> p g r u", g=2, u=2),
-                )
-            return grouped
+            return turn([[h[c][m][:].bitcast(F32)[:, u * P : (u + 1) * P] for u in range(2)] for m in range(MT)])
 
         def scale_y(m):
             for half in range(2):
@@ -213,82 +236,101 @@ def tile_psd_projection_dual_residual_s3_kernel(
                     scale=RHO,
                 )
 
-        def second_pass(acc, m, j, g):
-            cols = slice(m * P, (m + 1) * P)
+        def second_pass(acc, m, first, width, g):
+            cols = slice((m % 2) * P, (m % 2 + 1) * P)
             nc.tensor.matmul_mx(
-                out=acc[:],
-                lhsT=h_codes[g][:, cols].bitcast(FP8X4),
-                lhsT_scale=h_scales[g][:, cols],
-                rhs=vt[g][:, 2 * j * W : 2 * (j + 1) * W].bitcast(FP4X4),
-                rhs_scale=vt_plane[:, g, j * W : (j + 1) * W],
+                out=acc[1][:, 0:width],
+                lhsT=h_codes[g][m // 2][:, cols].bitcast(FP8X4),
+                lhsT_scale=h_scales[g][m // 2][:, cols],
+                rhs=vt[g][:, 2 * first : 2 * (first + width)].bitcast(FP4X4),
+                rhs_scale=vt_plane[:, g, first : first + width],
                 start=(g == 0),
                 stop=(g == NC - 1),
             )
 
-        def finish(acc, m, j):
+        def finish(acc, m, first, width):
             result = outs.tile([P, W], F32, name="result")
+            half, inside = divmod(first, N // 2)
             nc.vector.scalar_tensor_tensor(
-                out=result[:],
-                in0=acc[:],
+                out=result[:, 0:width],
+                in0=acc[1][:, 0:width],
                 scalar=RHO,
-                in1=y_rho[m][j // 2][:, (j % 2) * W : (j % 2 + 1) * W],
+                in1=y_rho[m][half][:, inside : inside + width],
                 op0=ALU.mult,
                 op1=ALU.subtract,
             )
-            nc.sync.dma_start(out=out[m * P : (m + 1) * P, j * W : (j + 1) * W], in_=result[:])
+            release(acc)
+            nc.sync.dma_start(out=out[m * P : (m + 1) * P, first : first + width], in_=result[:, 0:width])
 
-        nc.vector.tensor_scalar(out=lam_clip[:], in0=lam_raw[:], scalar1=FLOOR, scalar2=None, op0=ALU.max)
-        xg0 = turn_x(0)
+        accs = []
         spread_lam()
-        vg0 = interleave_v(0, True)
-        quantize(x_codes[0], x_scales[0], xg0)
-        quantize(v_codes[0], v_scales[0], vg0)
-        xg1 = turn_x(1)
-        quantize(x_codes[1], x_scales[1], xg1)
-        acc0 = first_stage(0, 0)
-        acc1 = first_stage(0, 1)
-        weigh(0, 0, acc0)
-        xg2 = turn_x(2)
-        xg3 = turn_x(3)
-        weigh(0, 1, acc1)
-        vg1 = interleave_v(1, True)
-        quantize(x_codes[2], x_scales[2], xg2)
-        quantize(v_codes[1], v_scales[1], vg1)
-        quantize(x_codes[3], x_scales[3], xg3)
-        for m in range(2, MT):
-            weigh(0, m, first_stage(0, m))
+        w0 = sort_words(xr[0], GR)
+        g0 = turn(w0)
+        w1 = sort_words(xr[1], GR)
+        g1 = turn(w1)
+        quantize_pair(xr_codes[0], xr_scales[0], g0)
+        w2 = sort_words(xr[2], GR)
+        quantize_pair(xr_codes[1], xr_scales[1], g1)
+        accs.append(rest_passes(0, 0))
+        g2 = turn(w2)
+        w3 = sort_words(xr[3], GR)
+        wt = sort_words(xt, MT)
+        accs.append(rest_passes(0, 1))
+        quantize_pair(xr_codes[2], xr_scales[2], g2)
+        g3 = turn(w3)
+        gt = turn(wt)
+        vg = interleave_v(0, True)
+        accs.append(rest_passes(0, 2))
+        quantize_pair(xr_codes[3], xr_scales[3], g3)
+        accs.append(rest_passes(0, 3))
+        quantize(xt_codes[0], xt_scales[0], gt[0])
+        quantize(v_codes[0], v_scales[0], vg)
+        quantize(xt_codes[1], xt_scales[1], gt[1])
 
-        for c in range(1, NC):
-            if c + 1 < NC:
-                vg = interleave_v(c + 1, False)
-            weigh(c, 0, first_stage(c, 0))
-            weigh(c, 1, first_stage(c, 1))
+        vg = interleave_v(1, False)
+        ahead = [rest_passes(1, m) for m in range(2)]
+        for m in range(MT):
+            top_pass(0, m, accs[m])
+            if m == 1:
+                quantize(v_codes[1], v_scales[1], vg)
+        for c in range(1, NC - 1):
+            vg = interleave_v(c + 1, False)
+            accs = ahead + [rest_passes(c, m) for m in range(len(ahead), MT)]
+            ahead = []
+            for m in range(MT):
+                top_pass(c, m, accs[m])
+                if m == 1:
+                    quantize(v_codes[c + 1], v_scales[c + 1], vg)
             hg = turn_h(c - 1)
-            if c + 1 < NC:
-                quantize(v_codes[c + 1], v_scales[c + 1], vg)
-            else:
+            quantize_pair(h_codes[c - 1], h_scales[c - 1], hg)
+        c = NC - 1
+        for m in range(MT):
+            if m == 2:
+                hg = turn_h(c - 1)
                 scale_y(0)
-            weigh(c, 2, first_stage(c, 2))
-            quantize(h_codes[c - 1], h_scales[c - 1], hg)
-            weigh(c, 3, first_stage(c, 3))
+            top_pass(c, m, rest_passes(c, m))
+            if m == 2:
+                quantize_pair(h_codes[c - 1], h_scales[c - 1], hg)
 
         accs = []
         for j in range(NC):
-            if j == 2:
-                hg = turn_h(NC - 1)
-                quantize(h_codes[NC - 1], h_scales[NC - 1], hg)
+            if j == 1:
+                quantize_pair(h_codes[NC - 1], h_scales[NC - 1], turn_h(NC - 1))
                 scale_y(1)
             accs.append(bank())
             for g in range(NC - 1):
-                second_pass(accs[j], 0, j, g)
+                second_pass(accs[j], 0, j * W, W, g)
         for j in range(NC):
-            second_pass(accs[j], 0, j, NC - 1)
-            finish(accs[j], 0, j)
+            second_pass(accs[j], 0, j * W, W, NC - 1)
+            finish(accs[j], 0, j * W, W)
         for m in range(1, MT):
             if m + 1 < MT:
                 scale_y(m + 1)
-            for j in range(NC):
+            pieces = [(j * W, W) for j in range(NC)]
+            if m == MT - 1:
+                pieces = pieces[:-1] + [(N - W + q * P, P) for q in range(4)]
+            for first, width in pieces:
                 acc = bank()
                 for g in range(NC):
-                    second_pass(acc, m, j, g)
-                finish(acc, m, j)
+                    second_pass(acc, m, first, width, g)
+                finish(acc, m, first, width)

@@ -111,22 +111,24 @@ def tile_psd_projection_dual_residual_s3_kernel(
 
         load_x_rest(0)
         load_x_rest(1)
-        load_plane(vr_planes[0], v_rest_scales, 0, W)
+        load_plane(vr_planes[0], v_rest_scales, 0 * W, 1 * W)
         load_v_rest(0)
         load_x_rest(2)
         load_x_rest(3)
         nc.sync.dma_start(out=xt[:].rearrange("p (m k) -> p m k", m=MT), in_=x_top.rearrange("(m p) k -> p m k", p=P))
         load_v_top(0)
-        for c in range(1, NC):
-            if c < 3:
-                load_plane(vr_planes[c], v_rest_scales, c * W, N if c == 2 else (c + 1) * W)
-            load_v_rest(c)
-            load_v_top(c)
+        load_plane(vr_planes[1], v_rest_scales, 1 * W, 2 * W)
+        load_v_rest(1)
+        load_v_top(1)
+        load_v_top(2)
+        load_plane(vr_planes[2], v_rest_scales, 2 * W, N)
+        load_v_rest(2)
+        load_v_rest(3)
+        load_v_top(3)
         load_plane(vt_plane, vt_scales, 0, N)
-        nc.sync.dma_start(out=y_raw[0][:], in_=y[0:P, :])
         for g in range(NC):
             nc.sync.dma_start(out=vt[g][:].bitcast(I32), in_=vt_words.bitcast(I32)[g])
-        for m in range(1, MT):
+        for m in range(MT):
             nc.sync.dma_start(out=y_raw[m][:], in_=y[m * P : (m + 1) * P, :])
 
         def sort_words(raw, blocks):
@@ -279,9 +281,9 @@ def tile_psd_projection_dual_residual_s3_kernel(
         quantize_pair(xr_codes[2], xr_scales[2], g2)
         g3 = turn(w3)
         gt = turn(wt)
-        vg = interleave_v(0, True)
         accs.append(rest_passes(0, 2))
         quantize_pair(xr_codes[3], xr_scales[3], g3)
+        vg = interleave_v(0, True)
         accs.append(rest_passes(0, 3))
         quantize(xt_codes[0], xt_scales[0], gt[0])
         quantize(v_codes[0], v_scales[0], vg)
@@ -307,7 +309,6 @@ def tile_psd_projection_dual_residual_s3_kernel(
         for m in range(MT):
             if m == 2:
                 hg = turn_h(c - 1)
-                scale_y(0)
             top_pass(c, m, rest_passes(c, m))
             if m == 2:
                 quantize_pair(h_codes[c - 1], h_scales[c - 1], hg)
@@ -316,6 +317,7 @@ def tile_psd_projection_dual_residual_s3_kernel(
         for j in range(NC):
             if j == 1:
                 quantize_pair(h_codes[NC - 1], h_scales[NC - 1], turn_h(NC - 1))
+                scale_y(0)
                 scale_y(1)
             accs.append(bank())
             for g in range(NC - 1):

from contextlib import ExitStack

import concourse.mybir as mybir
from concourse.masks import make_identity

M, KA, KB, N = 512, 512, 1536, 2048
FLOOR = 0.25
RHO = 1.5
FLOPS = 2 * M * (KA + KB) * N + 2 * M * N * N

F32 = mybir.dt.float32
BF16 = mybir.dt.bfloat16
I32 = mybir.dt.int32
U32 = mybir.dt.uint32
U8 = mybir.dt.uint8
FP8X4 = mybir.dt.float8_e4m3fn_x4
FP4X4 = mybir.dt.float4_e2m1fn_x4
ALU = mybir.AluOpType
ACT = mybir.ActivationFunctionType

P = 128
W = 512
MT = M // P
NC = N // W
GR = KB // W


def tile_psd_projection_dual_residual_s3_kernel(
    tc, x_top, x_rest, v_top, v_rest_words, v_rest_scales, lam, vt_words, vt_scales, y, out
):
    nc = tc.nc
    with ExitStack() as ctx:
        keep = ctx.enter_context(tc.tile_pool(name="keep", bufs=1))
        stage = ctx.enter_context(tc.tile_pool(name="stage", bufs=2))
        outs = ctx.enter_context(tc.tile_pool(name="outs", bufs=10))
        psum = ctx.enter_context(tc.psum_pool(name="psum", bufs=1))
        ctx.enter_context(tc.manual_schedule())

        def kept(name, shape, dtype):
            return keep.tile(shape, dtype, name=name, align_bytes=64)

        free_banks = list(range(8))

        def bank():
            number = free_banks[0]
            free_banks.remove(number)
            return number, psum.tile([P, W], F32, name="bank%d" % number)

        def release(held):
            free_banks.append(held[0])

        lam_raw = kept("lam_raw", [P, 16], BF16)
        lam_clip = kept("lam_clip", [P, 16], BF16)
        lam_all = kept("lam_all", [P, N], BF16)
        ident = kept("ident", [P, P], F32)
        xr = [kept("xr%d" % m, [P, KB], BF16) for m in range(MT)]
        xt = kept("xt", [P, MT * KA], BF16)
        xr_codes = [[kept("xc%d_%d" % (m, b), [P, (2 - b) * P], U32) for b in range(2)] for m in range(MT)]
        xr_scales = [[kept("xs%d_%d" % (m, b), [P, (2 - b) * P], U8) for b in range(2)] for m in range(MT)]
        xt_codes = [kept("xtc%d" % b, [P, 2 * P], U32) for b in range(2)]
        xt_scales = [kept("xts%d" % b, [P, 2 * P], U8) for b in range(2)]
        v_raw = [kept("vraw%d" % c, [P, 4, W], BF16) for c in range(NC)]
        v_codes = [kept("vc%d" % c, [P, W], U32) for c in range(NC)]
        v_scales = [kept("vs%d" % c, [P, W], U8) for c in range(NC)]
        vr = [kept("vr%d" % c, [P, GR, 2 * W], U8) for c in range(NC)]
        vr_planes = [kept("vrs%d" % i, [P, GR, width], U8) for i, width in enumerate((W, W, 2 * W))]
        vt = [kept("vt%d" % g, [P, 2 * N], U8) for g in range(NC)]
        vt_plane = kept("vts", [P, NC, N], U8)
        h = [[kept("h%d_%d" % (c, m), [P, W], BF16) for m in range(MT)] for c in range(NC)]
        h_codes = [[kept("hc%d_%d" % (c, b), [P, 2 * P], U32) for b in range(2)] for c in range(NC)]
        h_scales = [[kept("hs%d_%d" % (c, b), [P, 2 * P], U8) for b in range(2)] for c in range(NC)]
        y_raw = [kept("y%d" % m, [P, N], BF16) for m in range(MT)]
        y_rho = [[kept("yr%d_%d" % (m, half), [P, N // 2], F32) for half in range(2)] for m in range(MT)]

        def quantize(codes, scales, grouped):
            nc.vector.quantize_mx(out=codes[:].bitcast(FP8X4), scales=scales[:], in_=grouped[:])

        def clear(plane):
            nc.vector.memset(plane[:, :, :].rearrange("p g n -> p (g n)").bitcast(I32), 0)

        make_identity(nc, ident[:])
        clear(vr_planes[0])
        clear(vr_planes[1])
        clear(vr_planes[2])
        clear(vt_plane[:, 0:2, :])

        def load_v_top(c):
            nc.sync.dma_start(
                out=v_raw[c][:], in_=v_top.rearrange("(p j) n -> p j n", j=4)[:, :, c * W : (c + 1) * W]
            )

        def load_v_rest(c):
            nc.sync.dma_start(
                out=vr[c][:].bitcast(I32),
                in_=v_rest_words.bitcast(I32).rearrange("g p n -> p g n")[:, :, c * W // 2 : (c + 1) * W // 2],
            )

        def load_plane(plane, scales, first, last):
            for r in range(4):
                nc.sync.dma_start(
                    out=plane[:].bitcast(I32)[r:P:32, :, :],
                    in_=scales.bitcast(I32)[:, r:16:4, first // 4 : last // 4].rearrange("g q n -> q g n"),
                )

        nc.sync.dma_start(out=lam_raw[:], in_=lam.rearrange("(p c) -> p c", c=16))
        nc.vector.tensor_scalar(out=lam_clip[:], in0=lam_raw[:], scalar1=FLOOR, scalar2=None, op0=ALU.max)
        clear(vt_plane[:, 2:4, :])

        def load_x_rest(m):
            nc.sync.dma_start(out=xr[m][:], in_=x_rest[m * P : (m + 1) * P, :])

        load_x_rest(0)
        load_x_rest(1)
        load_plane(vr_planes[0], v_rest_scales, 0 * W, 1 * W)
        load_v_rest(0)
        load_x_rest(2)
        load_x_rest(3)
        nc.sync.dma_start(out=xt[:].rearrange("p (m k) -> p m k", m=MT), in_=x_top.rearrange("(m p) k -> p m k", p=P))
        load_v_top(0)
        load_plane(vr_planes[1], v_rest_scales, 1 * W, 2 * W)
        load_v_rest(1)
        load_v_top(1)
        load_v_top(2)
        load_plane(vr_planes[2], v_rest_scales, 2 * W, N)
        load_v_rest(2)
        load_v_rest(3)
        load_v_top(3)
        load_plane(vt_plane, vt_scales, 0, N)
        for g in range(NC):
            nc.sync.dma_start(out=vt[g][:].bitcast(I32), in_=vt_words.bitcast(I32)[g])
        for m in range(MT):
            nc.sync.dma_start(out=y_raw[m][:], in_=y[m * P : (m + 1) * P, :])

        def sort_words(raw, blocks):
            ordered = stage.tile([P, 2, blocks * P], F32, name="ordered", align_bytes=64, bufs=3)
            nc.vector.tensor_copy(
                out=ordered[:].rearrange("p u (a i) -> p a u i", i=4),
                in_=raw[:].bitcast(F32).rearrange("p (a i u) -> p a u i", i=4, u=2),
            )
            return [[ordered[:, u, s * P : (s + 1) * P] for u in range(2)] for s in range(blocks)]

        def turn(sources):
            banks = [bank(), bank()]
            for s in range(len(sources)):
                for u in range(2):
                    col = ((s % 2) * 2 + u) * P
                    nc.tensor.transpose(banks[s // 2][1][:, col : col + P], sources[s][u], ident[:])
            groups = []
            for b in range(2):
                blocks = min(2, len(sources) - 2 * b)
                grouped = stage.tile([P, blocks * W], BF16, name="grouped", align_bytes=64, bufs=6)
                nc.scalar.copy(
                    out=grouped[:].bitcast(F32).rearrange("p (s r u) -> p s r u", s=blocks, u=2),
                    in_=banks[b][1][:, 0 : blocks * 2 * P].rearrange("p (s u r) -> p s r u", s=blocks, u=2),
                )
                release(banks[b])
                groups.append(grouped)
            return groups

        def quantize_pair(codes, scales, groups):
            for b in range(2):
                quantize(codes[b], scales[b], groups[b])

        def interleave_v(c, on_vector):
            grouped = stage.tile([P, 4 * W], BF16, name="vg", align_bytes=64)
            dst = grouped[:].rearrange("p (c i t) -> p c t i", i=4, t=4)
            src = v_raw[c][:].rearrange("p t (c i) -> p c t i", i=4)
            if on_vector:
                nc.vector.tensor_copy(out=dst, in_=src)
            else:
                nc.scalar.copy(out=dst, in_=src)
            return grouped

        def spread_lam():
            words = lam_clip[:].bitcast(F32)
            banks = [bank(), bank()]
            for u in range(2):
                for b in range(4):
                    w = 2 * b + u
                    nc.tensor.transpose(
                        banks[u][1][:, b * P : (b + 1) * P], words[:, w : w + 1].to_broadcast([P, P]), ident[:]
                    )
            for u in range(2):
                nc.scalar.copy(
                    out=lam_all[:].bitcast(F32).rearrange("p (c u a b) -> p u c a b", c=NC, u=2, b=4)[:, u],
                    in_=banks[u][1][:].rearrange("p (b c a) -> p c a b", b=4, c=NC),
                )
                release(banks[u])

        def rest_passes(c, m):
            acc = bank()
            plane = vr_planes[min(c, 2)]
            first = W if c == 3 else 0
            for g in range(GR):
                cols = slice((g % 2) * P, (g % 2 + 1) * P)
                nc.tensor.matmul_mx(
                    out=acc[1][:],
                    lhsT=xr_codes[m][g // 2][:, cols].bitcast(FP8X4),
                    lhsT_scale=xr_scales[m][g // 2][:, cols],
                    rhs=vr[c][:, g, :].bitcast(FP4X4),
                    rhs_scale=plane[:, g, first : first + W],
                    start=(g == 0),
                    stop=False,
                )
            return acc

        def top_pass(c, m, acc):
            cols = slice((m % 2) * P, (m % 2 + 1) * P)
            nc.tensor.matmul_mx(
                out=acc[1][:],
                lhsT=xt_codes[m // 2][:, cols].bitcast(FP8X4),
                lhsT_scale=xt_scales[m // 2][:, cols],
                rhs=v_codes[c][:].bitcast(FP8X4),
                rhs_scale=v_scales[c][:],
                start=False,
                stop=True,
            )
            weigh(c, m, acc)

        def weigh(c, m, acc):
            nc.vector.tensor_tensor(
                out=h[c][m][:].rearrange("p (u q e) -> p u q e", u=2, e=2),
                in0=acc[1][:].rearrange("p (q u e) -> p u q e", u=2, e=2),
                in1=lam_all[:, c * W : (c + 1) * W].rearrange("p (u q e) -> p u q e", u=2, e=2),
                op=ALU.mult,
            )
            release(acc)

        def turn_h(c):
            return turn([[h[c][m][:].bitcast(F32)[:, u * P : (u + 1) * P] for u in range(2)] for m in range(MT)])

        def scale_y(m):
            for half in range(2):
                nc.scalar.activation(
                    out=y_rho[m][half][:],
                    in_=y_raw[m][:, half * (N // 2) : (half + 1) * (N // 2)],
                    func=ACT.Copy,
                    scale=RHO,
                )

        def second_pass(acc, m, first, width, g):
            cols = slice((m % 2) * P, (m % 2 + 1) * P)
            nc.tensor.matmul_mx(
                out=acc[1][:, 0:width],
                lhsT=h_codes[g][m // 2][:, cols].bitcast(FP8X4),
                lhsT_scale=h_scales[g][m // 2][:, cols],
                rhs=vt[g][:, 2 * first : 2 * (first + width)].bitcast(FP4X4),
                rhs_scale=vt_plane[:, g, first : first + width],
                start=(g == 0),
                stop=(g == NC - 1),
            )

        def finish(acc, m, first, width):
            result = outs.tile([P, W], F32, name="result")
            half, inside = divmod(first, N // 2)
            nc.vector.scalar_tensor_tensor(
                out=result[:, 0:width],
                in0=acc[1][:, 0:width],
                scalar=RHO,
                in1=y_rho[m][half][:, inside : inside + width],
                op0=ALU.mult,
                op1=ALU.subtract,
            )
            release(acc)
            nc.sync.dma_start(out=out[m * P : (m + 1) * P, first : first + width], in_=result[:, 0:width])

        accs = []
        spread_lam()
        w0 = sort_words(xr[0], GR)
        g0 = turn(w0)
        w1 = sort_words(xr[1], GR)
        g1 = turn(w1)
        quantize_pair(xr_codes[0], xr_scales[0], g0)
        w2 = sort_words(xr[2], GR)
        quantize_pair(xr_codes[1], xr_scales[1], g1)
        accs.append(rest_passes(0, 0))
        g2 = turn(w2)
        w3 = sort_words(xr[3], GR)
        wt = sort_words(xt, MT)
        accs.append(rest_passes(0, 1))
        quantize_pair(xr_codes[2], xr_scales[2], g2)
        g3 = turn(w3)
        gt = turn(wt)
        accs.append(rest_passes(0, 2))
        quantize_pair(xr_codes[3], xr_scales[3], g3)
        vg = interleave_v(0, True)
        accs.append(rest_passes(0, 3))
        quantize(xt_codes[0], xt_scales[0], gt[0])
        quantize(v_codes[0], v_scales[0], vg)
        quantize(xt_codes[1], xt_scales[1], gt[1])

        vg = interleave_v(1, False)
        ahead = [rest_passes(1, m) for m in range(2)]
        for m in range(MT):
            top_pass(0, m, accs[m])
            if m == 1:
                quantize(v_codes[1], v_scales[1], vg)
        for c in range(1, NC - 1):
            vg = interleave_v(c + 1, False)
            accs = ahead + [rest_passes(c, m) for m in range(len(ahead), MT)]
            ahead = []
            for m in range(MT):
                top_pass(c, m, accs[m])
                if m == 1:
                    quantize(v_codes[c + 1], v_scales[c + 1], vg)
            hg = turn_h(c - 1)
            quantize_pair(h_codes[c - 1], h_scales[c - 1], hg)
        c = NC - 1
        for m in range(MT):
            if m == 2:
                hg = turn_h(c - 1)
            top_pass(c, m, rest_passes(c, m))
            if m == 2:
                quantize_pair(h_codes[c - 1], h_scales[c - 1], hg)

        accs = []
        for j in range(NC):
            if j == 1:
                quantize_pair(h_codes[NC - 1], h_scales[NC - 1], turn_h(NC - 1))
                scale_y(0)
                scale_y(1)
            accs.append(bank())
            for g in range(NC - 1):
                second_pass(accs[j], 0, j * W, W, g)
        for j in range(NC):
            second_pass(accs[j], 0, j * W, W, NC - 1)
            finish(accs[j], 0, j * W, W)
        for m in range(1, MT):
            if m + 1 < MT:
                scale_y(m + 1)
            pieces = [(j * W, W) for j in range(NC)]
            if m == MT - 1:
                pieces = pieces[:-1] + [(N - W + q * P, P) for q in range(4)]
            for first, width in pieces:
                acc = bank()
                for g in range(NC):
                    second_pass(acc, m, first, width, g)
                finish(acc, m, first, width)
